import numpy as np
import ml_dtypes


def mxq(x, axis, fmt="e4m3"):
    dtype, down = {"e4m3": (ml_dtypes.float8_e4m3fn, 7), "e5m2": (ml_dtypes.float8_e5m2, 14)}[fmt]
    v = np.moveaxis(np.asarray(x, np.float32).astype(ml_dtypes.bfloat16).astype(np.float64), axis, -1)
    blocks = v.reshape(v.shape[:-1] + (-1, 32))
    amax = np.abs(blocks).max(-1, keepdims=True)
    byte = np.maximum(np.where(amax > 0, np.frexp(amax)[1] - 1 + 127, 0) - down, 1)
    scale = np.exp2(byte - 127.0)
    codes = (blocks / scale).astype(np.float32).astype(dtype).astype(np.float64)
    return np.moveaxis((codes * scale).reshape(v.shape), -1, axis)


WIDE = False


def mx_kscale(k):
    if not WIDE:
        return np.ones(k)
    levels = np.array([10, -10, 5, -5, 0])
    if k % 512:
        return np.exp2(np.random.permutation(np.resize(levels, k // 32))).repeat(32)
    a = np.empty((k // 512, 16))
    for p in range(k // 512):
        a[p, :8] = np.random.permutation(np.resize(levels, 8))
        for g in range(8):
            far = levels[np.abs(levels - a[p, g]) >= 10]
            a[p, g + 8] = far[np.random.randint(len(far))]
    return np.exp2(a.ravel()).repeat(32)


def f64(x):
    return np.asarray(x).astype(np.float64)


def striped(idx):
    return np.tile(idx.reshape(-1, 16).T, (8, 1)).astype(np.uint16)


def unstriped(offs):
    return offs[:16].T.reshape(-1).astype(np.int64)


def pack_weight(w):
    k, n = w.shape
    w = f64(np.asarray(w, np.float32).astype(ml_dtypes.bfloat16)).reshape(k // 32, 32, n)
    amax = np.abs(w).max(1)
    byte = np.clip(np.where(amax > 0, np.frexp(amax)[1] - 1 + 127 - 7, 1), 1, 254)
    scaled = (w * np.exp2(127.0 - byte)[:, None, :]).reshape(k, n).astype(np.float32)
    words = np.ascontiguousarray(scaled.reshape(k // 512, 128, 4, n).transpose(0, 1, 3, 2)).astype(ml_dtypes.float8_e4m3fn).view(np.uint8)
    return words, np.ascontiguousarray(byte.astype(np.uint8).reshape(k // 512, 16, n))


def unpack_weight(words, scales):
    g, p, n, _ = words.shape
    vals = np.ascontiguousarray(words).view(ml_dtypes.float8_e4m3fn).astype(np.float64) * np.repeat(np.exp2(scales.astype(np.float64) - 127.0), 8, axis=1)[..., None]
    return vals.transpose(0, 1, 3, 2).reshape(g * 512, n)


def planes(y):
    n, m = y.shape
    v = y.astype(np.float32).astype(ml_dtypes.bfloat16).astype(np.float64).reshape(n // 32, 32, m)
    top = np.abs(v).max(1)
    byte = np.clip(np.where(top > 0, np.frexp(top)[1] - 1 + 127 - 7, 1), 1, 254)
    codes = (v * np.exp2(127.0 - byte)[:, None, :]).reshape(n, m).astype(np.float32).astype(ml_dtypes.float8_e4m3fn).view(np.uint8)
    words = codes.reshape(n // 512, 128, 4, m).transpose(0, 1, 3, 2)
    return np.ascontiguousarray(words), np.ascontiguousarray(byte.astype(np.uint8).reshape(n // 512, 16, m))


def gelu(v):
    return 0.5 * v * (1.0 + np.tanh(np.sqrt(2.0 / np.pi) * (v + 0.044715 * v**3)))


K, T, S, N = 1024, 4096, 1024, 512


def setup_inputs():
    n = np.random.standard_normal
    s = mx_kscale(K)[:, None]
    packed_xT = pack_weight(n((K, T)) * s)
    return {
        "x_words": packed_xT[0],
        "x_scales": packed_xT[1],
        "w1": (n((K, N)) / np.sqrt(K) / s).astype(np.float32),
        "w2": (n((K, N)) / np.sqrt(K) / s).astype(np.float32),
        "feat": (n((N, S))).astype(np.float32),
        "offs": striped(np.random.permutation(T)[:S]),
    }


def reference(x_words, x_scales, w1, w2, feat, offs):
    xq = unpack_weight(x_words, x_scales)[:, unstriped(offs)]
    g = mxq(f64(w1), 0, "e4m3").T @ xq
    h = mxq(f64(w2), 0, "e4m3").T @ xq
    out_0 = gelu(f64(feat) + f64(feat) * g + h)
    return (out_0,) + planes(out_0)

@@ -1,0 +1,176 @@
+from contextlib import ExitStack
+
+import concourse.mybir as mybir
+
+K, T, S, N = 1024, 4096, 1024, 512
+FLOPS = 2 * 2 * K * N * S
+
+F32 = mybir.dt.float32
+BF16 = mybir.dt.bfloat16
+I32 = mybir.dt.int32
+U32 = mybir.dt.uint32
+U16 = mybir.dt.uint16
+U8 = mybir.dt.uint8
+FP8X4 = mybir.dt.float8_e4m3fn_x4
+ADD = mybir.AluOpType.add
+MULT = mybir.AluOpType.mult
+GELU = mybir.ActivationFunctionType.Gelu_apprx_tanh
+
+P = 128
+PACK = 4
+PASSES = K // (P * PACK)
+HALF = S // 2
+
+
+def tile_picked_zfilm_gelu_po_kernel(
+    tc, x_words, x_scales, w1, w2, feat, offs, out_0, out_1, out_2
+):
+    nc = tc.nc
+    with ExitStack() as ctx:
+        keep = ctx.enter_context(tc.tile_pool(name="keep", bufs=1))
+        psum = ctx.enter_context(tc.psum_pool(name="psum", bufs=1))
+
+        offsets = keep.tile([P, S // 16], U16, name="offsets")
+        nc.sync.dma_start(offsets[:], offs)
+
+        warm = keep.tile([P, 8], F32, name="warm")
+        warm2 = keep.tile([P, 8], F32, name="warm2")
+        nc.gpsimd.memset(warm[:], 0.0)
+        nc.scalar.activation(warm2[:], warm[:], GELU)
+
+        scale_table = keep.tile([P, T], U8, name="scale_table")
+        nc.vector.memset(scale_table[:].bitcast(I32), 0)
+
+        x_codes = []
+        for g in range(PASSES):
+            table = keep.tile([P, T], I32, name=f"word_table{g}")
+            nc.sync.dma_start(table[:], x_words[g].rearrange("p c r -> p (c r)").bitcast(I32))
+            if g == 0:
+                for q in range(4):
+                    nc.sync.dma_start(
+                        scale_table[32 * q : 32 * q + 4 * PASSES, :].bitcast(I32),
+                        x_scales[:, 4 * q : 4 * q + 4, :].bitcast(I32),
+                    )
+            picked = keep.tile([P, S], U32, name=f"x_codes{g}", align_bytes=64)
+            nc.vector.tensor_copy(picked[:], table[:].bitcast(U32).indirect(offsets[:]))
+            x_codes.append(picked)
+        x_planes = keep.tile([P, S], U8, name="x_planes", align_bytes=64)
+        nc.vector.tensor_copy(x_planes[:], scale_table[:].indirect(offsets[:]))
+
+        def load_weight(w, g, name):
+            raw = keep.tile([P, PACK, N], F32, name=f"{name}_raw{g}")
+            nc.sync.dma_start(raw[:], w[g * 512 : (g + 1) * 512, :].rearrange("(p j) c -> p j c", j=PACK))
+            return raw
+
+        def quantise_weight(raw, name):
+            src = raw[:].rearrange("p j (m t) -> p m j t", t=PACK)
+            pairs = []
+            for u in range(2):
+                dealt = keep.tile([P, 2, P, PACK], BF16, name=f"{name}_dealt{u}", align_bytes=64)
+                dst = dealt[:].rearrange("p t m j -> p m j t")
+                if u == 0:
+                    nc.vector.tensor_copy(dst, src[:, :, :, 0:2])
+                else:
+                    nc.scalar.copy(dst, src[:, :, :, 2:4])
+                codes = keep.tile([P, 2 * P], U32, name=f"{name}_codes{u}", align_bytes=64)
+                plane = keep.tile([P, 2 * P], U8, name=f"{name}_plane{u}", align_bytes=64)
+                nc.vector.quantize_mx(
+                    out=codes[:].bitcast(FP8X4), scales=plane[:], in_=dealt[:].rearrange("p t m j -> p (t m j)")
+                )
+                pairs.append((codes, plane))
+            return pairs
+
+        def product_pass(acc, pairs, g, t, cols):
+            codes, plane = pairs[t // 2]
+            m = slice((t % 2) * P, (t % 2 + 1) * P)
+            nc.tensor.matmul_mx(
+                out=acc[:],
+                lhsT=codes[:, m].bitcast(FP8X4),
+                lhsT_scale=plane[:, m],
+                rhs=x_codes[g][:, cols].bitcast(FP8X4),
+                rhs_scale=x_planes[4 * g : P, cols],
+                start=(g == 0),
+                stop=(g == PASSES - 1),
+            )
+
+        halves = [slice(0, HALF), slice(HALF, S)]
+        feat_rows = feat.rearrange("(p t) s -> p t s", t=PACK)
+        out_rows = out_0.rearrange("(p t) s -> p t s", t=PACK)
+
+        w1_raw = [load_weight(w1, g, "w1") for g in range(PASSES)]
+        feat_a = keep.tile([P, PACK, HALF], F32, name="feat_a")
+        nc.sync.dma_start(feat_a[:], feat_rows[:, :, halves[0]])
+        w2_raw = [load_weight(w2, g, "w2") for g in range(PASSES)]
+        feat_b = []
+        for t in range(PACK):
+            piece = keep.tile([P, HALF], F32, name=f"feat_b{t}")
+            nc.sync.dma_start(piece[:], feat_rows[:, t, halves[1]])
+            feat_b.append(piece)
+        feat_of = [[feat_a[:, t, :] for t in range(PACK)], [feat_b[t][:] for t in range(PACK)]]
+
+        g_acc = [
+            [psum.tile([P, HALF], F32, name=f"g{a}{t}", tag=f"bank{a}{t}") for t in range(PACK)] for a in range(2)
+        ]
+        for g in range(PASSES):
+            pairs = quantise_weight(w1_raw[g], f"w1_{g}")
+            for a in range(2):
+                for t in range(PACK):
+                    product_pass(g_acc[a][t], pairs, g, t, halves[a])
+
+        scaled = [[keep.tile([P, HALF], F32, name=f"scaled{a}{t}") for t in range(PACK)] for a in range(2)]
+
+        def modulate(a, t):
+            nc.vector.scalar_tensor_tensor(scaled[a][t][:], g_acc[a][t][:], 1.0, feat_of[a][t], ADD, MULT)
+
+        for t in range(PACK):
+            modulate(0, t)
+
+        w2_pairs = [quantise_weight(w2_raw[g], f"w2_{g}") for g in range(PASSES)]
+
+        y_planes = keep.tile([P, S], U8, name="y_planes", align_bytes=64)
+        words_out = out_1[0].rearrange("p c r -> p (c r)").bitcast(I32)
+
+        def shift_products(a):
+            h_acc = [psum.tile([P, HALF], F32, name=f"h{a}{t}", tag=f"bank{a}{t}") for t in range(PACK)]
+            for g in range(PASSES):
+                for t in range(PACK):
+                    product_pass(h_acc[t], w2_pairs[g], g, t, halves[a])
+            return h_acc
+
+        def finish(a, h_acc):
+            y = keep.tile([P, PACK, HALF], F32, name=f"y{a}")
+            for t in range(PACK):
+                u = keep.tile([P, HALF], F32, name=f"u{a}{t}")
+                nc.vector.tensor_tensor(u[:], h_acc[t][:], scaled[a][t][:], ADD)
+                nc.scalar.activation(y[:, t, :], u[:], GELU)
+                nc.sync.dma_start(out_rows[:, t, halves[a]], y[:, t, :])
+            return y
+
+        def hand_on(a, y, vector_cols):
+            woven = keep.tile([P, HALF, PACK], BF16, name=f"woven{a}", align_bytes=64)
+            dst = woven[:].rearrange("p (c i) t -> p c t i", i=4)
+            src = y[:].rearrange("p t (c i) -> p c t i", i=4)
+            c = vector_cols // 4
+            if c:
+                nc.vector.tensor_copy(dst[:, :c], src[:, :c])
+            nc.scalar.copy(dst[:, c:], src[:, c:])
+            y_codes = keep.tile([P, HALF], I32, name=f"y_codes{a}", align_bytes=64)
+            nc.vector.quantize_mx(
+                out=y_codes[:].bitcast(FP8X4),
+                scales=y_planes[:, halves[a]],
+                in_=woven[:].rearrange("p c t -> p (c t)"),
+            )
+            nc.sync.dma_start(words_out[:, halves[a]], y_codes[:])
+
+        y_a = finish(0, shift_products(0))
+        for t in range(PACK):
+            modulate(1, t)
+        h_b = shift_products(1)
+        hand_on(0, y_a, 0)
+        y_b = finish(1, h_b)
+        hand_on(1, y_b, 320)
+        for q in range(4):
+            queue = nc.sync if q % 2 else nc.scalar
+            queue.dma_start(
+                out_2[0, 4 * q : 4 * q + 4, :].bitcast(I32), y_planes[32 * q : 32 * q + 4, :].bitcast(I32)
+            )

@@ -14,6 +14,7 @@ U8 = mybir.dt.uint8
 FP8X4 = mybir.dt.float8_e4m3fn_x4
 ADD = mybir.AluOpType.add
 MULT = mybir.AluOpType.mult
+IDENTITY = mybir.ActivationFunctionType.Identity
 GELU = mybir.ActivationFunctionType.Gelu_apprx_tanh
 
 P = 128
@@ -39,34 +40,41 @@ def tile_picked_zfilm_gelu_po_kernel(
         nc.scalar.activation(warm2[:], warm[:], GELU)
 
         scale_table = keep.tile([P, T], U8, name="scale_table")
-        nc.vector.memset(scale_table[:].bitcast(I32), 0)
+        nc.sync.dma_start(scale_table[0:32, :].bitcast(I32), x_scales.rearrange("g q c -> (g q) c").bitcast(I32))
+        nc.vector.memset(scale_table[32:64, :].bitcast(I32), 0)
+        nc.vector.memset(scale_table[64:P, :].bitcast(I32), 0)
+        picked_rows = keep.tile([P, S], U8, name="picked_rows")
+        nc.vector.tensor_copy(picked_rows[:], scale_table[:].indirect(offsets[:]))
+        x_planes = []
+        for g in range(PASSES):
+            plane = keep.tile([P, S], U8, name=f"x_plane{g}", align_bytes=64)
+            nc.gpsimd.memset(plane[:].bitcast(I32), 0)
+            x_planes.append(plane)
+        for g in range(PASSES):
+            for q in range(4):
+                first = 16 * g + 4 * q
+                nc.gpsimd.dma_start(
+                    x_planes[g][32 * q : 32 * q + 4, :].bitcast(I32), picked_rows[first : first + 4, :].bitcast(I32)
+                )
 
         x_codes = []
         for g in range(PASSES):
             table = keep.tile([P, T], I32, name=f"word_table{g}")
             nc.sync.dma_start(table[:], x_words[g].rearrange("p c r -> p (c r)").bitcast(I32))
-            if g == 0:
-                for q in range(4):
-                    nc.sync.dma_start(
-                        scale_table[32 * q : 32 * q + 4 * PASSES, :].bitcast(I32),
-                        x_scales[:, 4 * q : 4 * q + 4, :].bitcast(I32),
-                    )
             picked = keep.tile([P, S], U32, name=f"x_codes{g}", align_bytes=64)
             nc.vector.tensor_copy(picked[:], table[:].bitcast(U32).indirect(offsets[:]))
             x_codes.append(picked)
-        x_planes = keep.tile([P, S], U8, name="x_planes", align_bytes=64)
-        nc.vector.tensor_copy(x_planes[:], scale_table[:].indirect(offsets[:]))
 
         def load_weight(w, g, name):
             raw = keep.tile([P, PACK, N], F32, name=f"{name}_raw{g}")
             nc.sync.dma_start(raw[:], w[g * 512 : (g + 1) * 512, :].rearrange("(p j) c -> p j c", j=PACK))
             return raw
 
-        def quantise_weight(raw, name):
+        def quantise_weight(raw, name, tags):
             src = raw[:].rearrange("p j (m t) -> p m j t", t=PACK)
             pairs = []
             for u in range(2):
-                dealt = keep.tile([P, 2, P, PACK], BF16, name=f"{name}_dealt{u}", align_bytes=64)
+                dealt = keep.tile([P, 2, P, PACK], BF16, name=f"{name}_dealt{u}", tag=tags[u], align_bytes=64)
                 dst = dealt[:].rearrange("p t m j -> p m j t")
                 if u == 0:
                     nc.vector.tensor_copy(dst, src[:, :, :, 0:2])
@@ -88,7 +96,7 @@ def tile_picked_zfilm_gelu_po_kernel(
                 lhsT=codes[:, m].bitcast(FP8X4),
                 lhsT_scale=plane[:, m],
                 rhs=x_codes[g][:, cols].bitcast(FP8X4),
-                rhs_scale=x_planes[4 * g : P, cols],
+                rhs_scale=x_planes[g][:, cols],
                 start=(g == 0),
                 stop=(g == PASSES - 1),
             )
@@ -98,7 +106,7 @@ def tile_picked_zfilm_gelu_po_kernel(
         out_rows = out_0.rearrange("(p t) s -> p t s", t=PACK)
 
         w1_raw = [load_weight(w1, g, "w1") for g in range(PASSES)]
-        feat_a = keep.tile([P, PACK, HALF], F32, name="feat_a")
+        feat_a = keep.tile([P, PACK, HALF], F32, name="feat_a", tag="after_modulate", align_bytes=64)
         nc.sync.dma_start(feat_a[:], feat_rows[:, :, halves[0]])
         w2_raw = [load_weight(w2, g, "w2") for g in range(PASSES)]
         feat_b = []
@@ -112,7 +120,7 @@ def tile_picked_zfilm_gelu_po_kernel(
             [psum.tile([P, HALF], F32, name=f"g{a}{t}", tag=f"bank{a}{t}") for t in range(PACK)] for a in range(2)
         ]
         for g in range(PASSES):
-            pairs = quantise_weight(w1_raw[g], f"w1_{g}")
+            pairs = quantise_weight(w1_raw[g], f"w1_{g}", [f"w1_{g}_0", f"w1_{g}_1"])
             for a in range(2):
                 for t in range(PACK):
                     product_pass(g_acc[a][t], pairs, g, t, halves[a])
@@ -122,19 +130,26 @@ def tile_picked_zfilm_gelu_po_kernel(
         def modulate(a, t):
             nc.vector.scalar_tensor_tensor(scaled[a][t][:], g_acc[a][t][:], 1.0, feat_of[a][t], ADD, MULT)
 
+        ones = keep.tile([P, 1], F32, name="ones", tag="after_gain", align_bytes=64)
+        nc.gpsimd.memset(ones[:], 1.0)
+        gain_b = [keep.tile([P, HALF], F32, name=f"gain_b{t}") for t in range(PACK)]
         for t in range(PACK):
             modulate(0, t)
+            nc.scalar.activation(gain_b[t][:], g_acc[1][t][:], IDENTITY, bias=ones[:])
 
-        w2_pairs = [quantise_weight(w2_raw[g], f"w2_{g}") for g in range(PASSES)]
+        w2_pairs = [quantise_weight(w2_raw[g], f"w2_{g}", ["after_modulate", "after_gain"]) for g in range(PASSES)]
 
         y_planes = keep.tile([P, S], U8, name="y_planes", align_bytes=64)
         words_out = out_1[0].rearrange("p c r -> p (c r)").bitcast(I32)
 
-        def shift_products(a):
-            h_acc = [psum.tile([P, HALF], F32, name=f"h{a}{t}", tag=f"bank{a}{t}") for t in range(PACK)]
+        def shift_products():
+            h_acc = [
+                [psum.tile([P, HALF], F32, name=f"h{a}{t}", tag=f"bank{a}{t}") for t in range(PACK)] for a in range(2)
+            ]
             for g in range(PASSES):
-                for t in range(PACK):
-                    product_pass(h_acc[t], w2_pairs[g], g, t, halves[a])
+                for a in range(2):
+                    for t in range(PACK):
+                        product_pass(h_acc[a][t], w2_pairs[g], g, t, halves[a])
             return h_acc
 
         def finish(a, h_acc):
@@ -153,7 +168,8 @@ def tile_picked_zfilm_gelu_po_kernel(
             c = vector_cols // 4
             if c:
                 nc.vector.tensor_copy(dst[:, :c], src[:, :c])
-            nc.scalar.copy(dst[:, c:], src[:, c:])
+            if c < HALF // 4:
+                nc.scalar.copy(dst[:, c:], src[:, c:])
             y_codes = keep.tile([P, HALF], I32, name=f"y_codes{a}", align_bytes=64)
             nc.vector.quantize_mx(
                 out=y_codes[:].bitcast(FP8X4),
@@ -162,13 +178,13 @@ def tile_picked_zfilm_gelu_po_kernel(
             )
             nc.sync.dma_start(words_out[:, halves[a]], y_codes[:])
 
-        y_a = finish(0, shift_products(0))
         for t in range(PACK):
-            modulate(1, t)
-        h_b = shift_products(1)
-        hand_on(0, y_a, 0)
-        y_b = finish(1, h_b)
-        hand_on(1, y_b, 320)
+            nc.gpsimd.tensor_tensor(scaled[1][t][:], gain_b[t][:], feat_of[1][t], MULT)
+        h_acc = shift_products()
+        y_a = finish(0, h_acc[0])
+        y_b = finish(1, h_acc[1])
+        hand_on(0, y_a, 512)
+        hand_on(1, y_b, 192)
         for q in range(4):
             queue = nc.sync if q % 2 else nc.scalar
             queue.dma_start(

@@ -39,7 +39,7 @@ def tile_picked_zfilm_gelu_po_kernel(
         nc.gpsimd.memset(warm[:], 0.0)
         nc.scalar.activation(warm2[:], warm[:], GELU)
 
-        scale_table = keep.tile([P, T], U8, name="scale_table")
+        scale_table = keep.tile([P, T], U8, name="scale_table", tag="after_modulate", align_bytes=64)
         nc.sync.dma_start(scale_table[0:32, :].bitcast(I32), x_scales.rearrange("g q c -> (g q) c").bitcast(I32))
         nc.vector.memset(scale_table[32:64, :].bitcast(I32), 0)
         nc.vector.memset(scale_table[64:P, :].bitcast(I32), 0)
@@ -53,33 +53,34 @@ def tile_picked_zfilm_gelu_po_kernel(
         for g in range(PASSES):
             for q in range(4):
                 first = 16 * g + 4 * q
-                nc.gpsimd.dma_start(
+                queue = nc.scalar if g == 0 else nc.gpsimd
+                queue.dma_start(
                     x_planes[g][32 * q : 32 * q + 4, :].bitcast(I32), picked_rows[first : first + 4, :].bitcast(I32)
                 )
 
         x_codes = []
         for g in range(PASSES):
-            table = keep.tile([P, T], I32, name=f"word_table{g}")
+            table = keep.tile([P, T], I32, name=f"word_table{g}", tag=f"table{g}")
             nc.sync.dma_start(table[:], x_words[g].rearrange("p c r -> p (c r)").bitcast(I32))
             picked = keep.tile([P, S], U32, name=f"x_codes{g}", align_bytes=64)
             nc.vector.tensor_copy(picked[:], table[:].bitcast(U32).indirect(offsets[:]))
             x_codes.append(picked)
 
-        def load_weight(w, g, name):
-            raw = keep.tile([P, PACK, N], F32, name=f"{name}_raw{g}")
+        def load_weight(w, g, name, tag):
+            raw = keep.tile([P, PACK, N], F32, name=f"{name}_raw{g}", tag=tag)
             nc.sync.dma_start(raw[:], w[g * 512 : (g + 1) * 512, :].rearrange("(p j) c -> p j c", j=PACK))
             return raw
 
         def quantise_weight(raw, name, tags):
-            src = raw[:].rearrange("p j (m t) -> p m j t", t=PACK)
+            src = raw[:].rearrange("p j (m t) -> p m t j", t=PACK)
             pairs = []
             for u in range(2):
                 dealt = keep.tile([P, 2, P, PACK], BF16, name=f"{name}_dealt{u}", tag=tags[u], align_bytes=64)
-                dst = dealt[:].rearrange("p t m j -> p m j t")
+                dst = dealt[:].rearrange("p t m j -> p m t j")
                 if u == 0:
-                    nc.vector.tensor_copy(dst, src[:, :, :, 0:2])
+                    nc.vector.tensor_copy(dst, src[:, :, 0:2, :])
                 else:
-                    nc.scalar.copy(dst, src[:, :, :, 2:4])
+                    nc.scalar.copy(dst, src[:, :, 2:4, :])
                 codes = keep.tile([P, 2 * P], U32, name=f"{name}_codes{u}", align_bytes=64)
                 plane = keep.tile([P, 2 * P], U8, name=f"{name}_plane{u}", align_bytes=64)
                 nc.vector.quantize_mx(
@@ -105,16 +106,10 @@ def tile_picked_zfilm_gelu_po_kernel(
         feat_rows = feat.rearrange("(p t) s -> p t s", t=PACK)
         out_rows = out_0.rearrange("(p t) s -> p t s", t=PACK)
 
-        w1_raw = [load_weight(w1, g, "w1") for g in range(PASSES)]
+        w1_raw = [load_weight(w1, g, "w1", f"raw{g}") for g in range(PASSES)]
         feat_a = keep.tile([P, PACK, HALF], F32, name="feat_a", tag="after_modulate", align_bytes=64)
         nc.sync.dma_start(feat_a[:], feat_rows[:, :, halves[0]])
-        w2_raw = [load_weight(w2, g, "w2") for g in range(PASSES)]
-        feat_b = []
-        for t in range(PACK):
-            piece = keep.tile([P, HALF], F32, name=f"feat_b{t}")
-            nc.sync.dma_start(piece[:], feat_rows[:, t, halves[1]])
-            feat_b.append(piece)
-        feat_of = [[feat_a[:, t, :] for t in range(PACK)], [feat_b[t][:] for t in range(PACK)]]
+        w2_raw = [load_weight(w2, g, "w2", f"table{g}") for g in range(PASSES)]
 
         g_acc = [
             [psum.tile([P, HALF], F32, name=f"g{a}{t}", tag=f"bank{a}{t}") for t in range(PACK)] for a in range(2)
@@ -125,16 +120,19 @@ def tile_picked_zfilm_gelu_po_kernel(
                 for t in range(PACK):
                     product_pass(g_acc[a][t], pairs, g, t, halves[a])
 
-        scaled = [[keep.tile([P, HALF], F32, name=f"scaled{a}{t}") for t in range(PACK)] for a in range(2)]
+        feat_b = []
+        for t in range(PACK):
+            piece = keep.tile([P, HALF], F32, name=f"feat_b{t}", tag=f"w1_{t // 2}_{t % 2}", align_bytes=64)
+            nc.sync.dma_start(piece[:], feat_rows[:, t, halves[1]])
+            feat_b.append(piece[:])
 
-        def modulate(a, t):
-            nc.vector.scalar_tensor_tensor(scaled[a][t][:], g_acc[a][t][:], 1.0, feat_of[a][t], ADD, MULT)
+        scaled_a = keep.tile([P, PACK, HALF], F32, name="scaled_a")
 
         ones = keep.tile([P, 1], F32, name="ones", tag="after_gain", align_bytes=64)
         nc.gpsimd.memset(ones[:], 1.0)
         gain_b = [keep.tile([P, HALF], F32, name=f"gain_b{t}") for t in range(PACK)]
         for t in range(PACK):
-            modulate(0, t)
+            nc.vector.scalar_tensor_tensor(scaled_a[:, t, :], g_acc[0][t][:], 1.0, feat_a[:, t, :], ADD, MULT)
             nc.scalar.activation(gain_b[t][:], g_acc[1][t][:], IDENTITY, bias=ones[:])
 
         w2_pairs = [quantise_weight(w2_raw[g], f"w2_{g}", ["after_modulate", "after_gain"]) for g in range(PASSES)]
@@ -156,35 +154,41 @@ def tile_picked_zfilm_gelu_po_kernel(
             y = keep.tile([P, PACK, HALF], F32, name=f"y{a}")
             for t in range(PACK):
                 u = keep.tile([P, HALF], F32, name=f"u{a}{t}")
-                nc.vector.tensor_tensor(u[:], h_acc[t][:], scaled[a][t][:], ADD)
+                nc.vector.tensor_tensor(u[:], h_acc[t][:], scaled[a][t], ADD)
                 nc.scalar.activation(y[:, t, :], u[:], GELU)
                 nc.sync.dma_start(out_rows[:, t, halves[a]], y[:, t, :])
             return y
 
-        def hand_on(a, y, vector_cols):
-            woven = keep.tile([P, HALF, PACK], BF16, name=f"woven{a}", align_bytes=64)
-            dst = woven[:].rearrange("p (c i) t -> p c t i", i=4)
-            src = y[:].rearrange("p t (c i) -> p c t i", i=4)
-            c = vector_cols // 4
-            if c:
-                nc.vector.tensor_copy(dst[:, :c], src[:, :c])
-            if c < HALF // 4:
-                nc.scalar.copy(dst[:, c:], src[:, c:])
-            y_codes = keep.tile([P, HALF], I32, name=f"y_codes{a}", align_bytes=64)
+        def hand_on(y, first, cols, vector_cols, name):
+            width = cols.stop - cols.start
+            woven = keep.tile([P, width, PACK], BF16, name=f"woven{name}", align_bytes=64)
+            src = y[:, :, cols].rearrange("p t c -> p c t")
+            split = width - vector_cols
+            if split:
+                nc.scalar.copy(woven[:, :split, :], src[:, :split, :])
+            if vector_cols:
+                nc.vector.tensor_copy(woven[:, split:, :], src[:, split:, :])
+            y_codes = keep.tile([P, width], I32, name=f"y_codes{name}", align_bytes=64)
+            out_cols = slice(first + cols.start, first + cols.stop)
             nc.vector.quantize_mx(
                 out=y_codes[:].bitcast(FP8X4),
-                scales=y_planes[:, halves[a]],
+                scales=y_planes[:, out_cols],
                 in_=woven[:].rearrange("p c t -> p (c t)"),
             )
-            nc.sync.dma_start(words_out[:, halves[a]], y_codes[:])
+            nc.sync.dma_start(words_out[:, out_cols], y_codes[:])
 
-        for t in range(PACK):
-            nc.gpsimd.tensor_tensor(scaled[1][t][:], gain_b[t][:], feat_of[1][t], MULT)
+        scaled_b0 = keep.tile([P, HALF], F32, name="scaled_b0", tag="after_modulate", align_bytes=64)
+        nc.vector.tensor_tensor(scaled_b0[:], gain_b[0][:], feat_b[0], MULT)
+        scaled_b = keep.tile([P, PACK - 1, HALF], F32, name="scaled_b", tag="after_gain", align_bytes=64)
+        for t in range(1, PACK):
+            nc.gpsimd.tensor_tensor(scaled_b[:, t - 1, :], gain_b[t][:], feat_b[t], MULT)
+        scaled = [[scaled_a[:, t, :] for t in range(PACK)], [scaled_b0[:]] + [scaled_b[:, t, :] for t in range(PACK - 1)]]
         h_acc = shift_products()
         y_a = finish(0, h_acc[0])
         y_b = finish(1, h_acc[1])
-        hand_on(0, y_a, 512)
-        hand_on(1, y_b, 192)
+        hand_on(y_a, 0, slice(0, HALF), HALF, "a")
+        hand_on(y_b, HALF, slice(0, 256), 0, "b0")
+        hand_on(y_b, HALF, slice(256, HALF), 128, "b1")
         for q in range(4):
             queue = nc.sync if q % 2 else nc.scalar
             queue.dma_start(

@@ -19,8 +19,10 @@ GELU = mybir.ActivationFunctionType.Gelu_apprx_tanh
 
 P = 128
 PACK = 4
-PASSES = K // (P * PACK)
+K_PASS = P * PACK
+PASSES = K // K_PASS
 HALF = S // 2
+QUARTER = S // 4
 
 
 def tile_picked_zfilm_gelu_po_kernel(
@@ -28,169 +30,169 @@ def tile_picked_zfilm_gelu_po_kernel(
 ):
     nc = tc.nc
     with ExitStack() as ctx:
-        keep = ctx.enter_context(tc.tile_pool(name="keep", bufs=1))
+        sbuf = ctx.enter_context(tc.tile_pool(name="sbuf", bufs=1))
         psum = ctx.enter_context(tc.psum_pool(name="psum", bufs=1))
 
-        offsets = keep.tile([P, S // 16], U16, name="offsets")
+        def new_tile(shape, dtype, name, tag=None):
+            return sbuf.tile(shape, dtype, name=name, tag=tag or name, align_bytes=64)
+
+        offsets = new_tile([P, S // 16], U16, "offsets")
         nc.sync.dma_start(offsets[:], offs)
 
-        warm = keep.tile([P, 8], F32, name="warm")
-        warm2 = keep.tile([P, 8], F32, name="warm2")
-        nc.gpsimd.memset(warm[:], 0.0)
-        nc.scalar.activation(warm2[:], warm[:], GELU)
+        warm_in = new_tile([P, 8], F32, "warm_in")
+        warm_out = new_tile([P, 8], F32, "warm_out")
+        nc.gpsimd.memset(warm_in[:], 0.0)
+        nc.scalar.activation(warm_out[:], warm_in[:], GELU)
 
-        scale_table = keep.tile([P, T], U8, name="scale_table", tag="after_modulate", align_bytes=64)
+        scale_table = new_tile([P, T], U8, "scale_table")
         nc.sync.dma_start(scale_table[0:32, :].bitcast(I32), x_scales.rearrange("g q c -> (g q) c").bitcast(I32))
         nc.vector.memset(scale_table[32:64, :].bitcast(I32), 0)
         nc.vector.memset(scale_table[64:P, :].bitcast(I32), 0)
-        picked_rows = keep.tile([P, S], U8, name="picked_rows")
+        picked_rows = new_tile([P, S], U8, "picked_rows")
         nc.vector.tensor_copy(picked_rows[:], scale_table[:].indirect(offsets[:]))
-        x_planes = []
-        for g in range(PASSES):
-            plane = keep.tile([P, S], U8, name=f"x_plane{g}", align_bytes=64)
+        x_planes = [new_tile([P, S], U8, f"x_plane{g}") for g in range(PASSES)]
+        for plane in x_planes:
             nc.gpsimd.memset(plane[:].bitcast(I32), 0)
-            x_planes.append(plane)
-        for g in range(PASSES):
+        for g, queue in enumerate((nc.scalar, nc.gpsimd)):
             for q in range(4):
                 first = 16 * g + 4 * q
-                queue = nc.scalar if g == 0 else nc.gpsimd
                 queue.dma_start(
                     x_planes[g][32 * q : 32 * q + 4, :].bitcast(I32), picked_rows[first : first + 4, :].bitcast(I32)
                 )
 
-        x_codes = []
-        for g in range(PASSES):
-            table = keep.tile([P, T], I32, name=f"word_table{g}", tag=f"table{g}")
-            nc.sync.dma_start(table[:], x_words[g].rearrange("p c r -> p (c r)").bitcast(I32))
-            picked = keep.tile([P, S], U32, name=f"x_codes{g}", align_bytes=64)
-            nc.vector.tensor_copy(picked[:], table[:].bitcast(U32).indirect(offsets[:]))
-            x_codes.append(picked)
-
-        def load_weight(w, g, name, tag):
-            raw = keep.tile([P, PACK, N], F32, name=f"{name}_raw{g}", tag=tag)
-            nc.sync.dma_start(raw[:], w[g * 512 : (g + 1) * 512, :].rearrange("(p j) c -> p j c", j=PACK))
+        def load_weight(w, g, name):
+            raw = new_tile([P, PACK, N], F32, name)
+            nc.sync.dma_start(raw[:], w[g * K_PASS : (g + 1) * K_PASS, :].rearrange("(p j) c -> p j c", j=PACK))
             return raw
 
-        def quantise_weight(raw, name, tags):
-            src = raw[:].rearrange("p j (m t) -> p m t j", t=PACK)
-            pairs = []
-            for u in range(2):
-                dealt = keep.tile([P, 2, P, PACK], BF16, name=f"{name}_dealt{u}", tag=tags[u], align_bytes=64)
-                dst = dealt[:].rearrange("p t m j -> p m t j")
-                if u == 0:
-                    nc.vector.tensor_copy(dst, src[:, :, 0:2, :])
-                else:
-                    nc.scalar.copy(dst, src[:, :, 2:4, :])
-                codes = keep.tile([P, 2 * P], U32, name=f"{name}_codes{u}", align_bytes=64)
-                plane = keep.tile([P, 2 * P], U8, name=f"{name}_plane{u}", align_bytes=64)
-                nc.vector.quantize_mx(
-                    out=codes[:].bitcast(FP8X4), scales=plane[:], in_=dealt[:].rearrange("p t m j -> p (t m j)")
-                )
-                pairs.append((codes, plane))
-            return pairs
+        def deal(raw, u, name):
+            dealt = new_tile([P, 2, P, PACK], BF16, name)
+            src = raw[:].rearrange("p j (m t) -> p m j t", t=PACK)[:, :, :, 2 * u : 2 * u + 2]
+            copy = nc.scalar.copy if u else nc.vector.tensor_copy
+            copy(dealt[:].rearrange("p t m j -> p m j t"), src)
+            return dealt
 
-        def product_pass(acc, pairs, g, t, cols):
+        def quantise(dealt, name, tag=None):
+            codes = new_tile([P, 2 * P], U32, f"{name}_codes", tag)
+            plane = new_tile([P, 2 * P], U8, f"{name}_plane")
+            nc.vector.quantize_mx(
+                out=codes[:].bitcast(FP8X4), scales=plane[:], in_=dealt[:].rearrange("p t m j -> p (t m j)")
+            )
+            return codes, plane
+
+        def prepare(raw, name):
+            return [quantise(deal(raw, u, f"{name}_dealt{u}"), f"{name}_{u}") for u in range(2)]
+
+        halves = [slice(0, HALF), slice(HALF, S)]
+
+        def product_pass(acc, pairs, g, t, a):
             codes, plane = pairs[t // 2]
             m = slice((t % 2) * P, (t % 2 + 1) * P)
             nc.tensor.matmul_mx(
                 out=acc[:],
                 lhsT=codes[:, m].bitcast(FP8X4),
                 lhsT_scale=plane[:, m],
-                rhs=x_codes[g][:, cols].bitcast(FP8X4),
-                rhs_scale=x_planes[g][:, cols],
+                rhs=x_codes[g][:, halves[a]].bitcast(FP8X4),
+                rhs_scale=x_planes[g][:, halves[a]],
                 start=(g == 0),
                 stop=(g == PASSES - 1),
             )
 
-        halves = [slice(0, HALF), slice(HALF, S)]
-        feat_rows = feat.rearrange("(p t) s -> p t s", t=PACK)
-        out_rows = out_0.rearrange("(p t) s -> p t s", t=PACK)
+        def new_banks(name):
+            return [
+                [psum.tile([P, HALF], F32, name=f"{name}{a}{t}", tag=f"bank{a}{t}") for t in range(PACK)]
+                for a in range(2)
+            ]
 
-        w1_raw = [load_weight(w1, g, "w1", f"raw{g}") for g in range(PASSES)]
-        feat_a = keep.tile([P, PACK, HALF], F32, name="feat_a", tag="after_modulate", align_bytes=64)
-        nc.sync.dma_start(feat_a[:], feat_rows[:, :, halves[0]])
-        w2_raw = [load_weight(w2, g, "w2", f"table{g}") for g in range(PASSES)]
-
-        g_acc = [
-            [psum.tile([P, HALF], F32, name=f"g{a}{t}", tag=f"bank{a}{t}") for t in range(PACK)] for a in range(2)
-        ]
+        x_codes, w1_raw = [], []
         for g in range(PASSES):
-            pairs = quantise_weight(w1_raw[g], f"w1_{g}", [f"w1_{g}_0", f"w1_{g}_1"])
-            for a in range(2):
+            table = new_tile([P, T], I32, f"word_table{g}")
+            nc.sync.dma_start(table[:], x_words[g].rearrange("p c r -> p (c r)").bitcast(I32))
+            w1_raw.append(load_weight(w1, g, f"w1_raw{g}"))
+            picked = new_tile([P, S], U32, f"x_codes{g}")
+            nc.vector.tensor_copy(picked[:], table[:].bitcast(U32).indirect(offsets[:]))
+            x_codes.append(picked)
+
+        feat_rows = feat.rearrange("(p t) s -> p t s", t=PACK)
+
+        def load_feat(a):
+            pieces = [new_tile([P, HALF], F32, f"feat{a}{t}") for t in range(PACK)]
+            for t in range(PACK):
+                nc.sync.dma_start(pieces[t][:], feat_rows[:, t, halves[a]])
+            return pieces
+
+        w2_raw, feats = [], []
+        for g in range(PASSES):
+            w2_raw.append(load_weight(w2, g, f"w2_raw{g}"))
+            feats.append(load_feat(g))
+
+        g_acc = new_banks("g")
+        for g in range(PASSES):
+            pairs = prepare(w1_raw[g], f"w1_{g}")
+            for t in range(PACK):
+                for a in range(2):
+                    product_pass(g_acc[a][t], pairs, g, t, a)
+
+        w2_pairs = [prepare(w2_raw[0], "w2_0")]
+
+        scaled_a = new_tile([P, PACK, HALF], F32, "scaled_a")
+        gains = [new_tile([P, HALF], F32, f"gain{t}") for t in range(PACK)]
+        for t in range(PACK):
+            nc.vector.scalar_tensor_tensor(scaled_a[:, t, :], g_acc[0][t][:], 1.0, feats[0][t][:], ADD, MULT)
+            nc.scalar.activation(gains[t][:], g_acc[1][t][:], IDENTITY, bias=1.0)
+
+        dealt = [deal(w2_raw[1], u, f"w2_1_dealt{u}") for u in range(2)]
+        first_pair = quantise(dealt[0], "w2_1_0")
+        scaled_b0 = new_tile([P, HALF], F32, "scaled_b0", "w2_1_dealt0")
+        nc.vector.tensor_tensor(scaled_b0[:], gains[0][:], feats[1][0][:], MULT)
+        w2_pairs.append([first_pair, quantise(dealt[1], "w2_1_1", "gain0")])
+        scaled_b = new_tile([P, PACK - 1, HALF], F32, "scaled_b", "w2_1_dealt1")
+        for t in range(1, PACK):
+            nc.gpsimd.tensor_tensor(scaled_b[:, t - 1, :], gains[t][:], feats[1][t][:], MULT)
+        scaled = [
+            [scaled_a[:, t, :] for t in range(PACK)],
+            [scaled_b0[:]] + [scaled_b[:, t, :] for t in range(PACK - 1)],
+        ]
+
+        h_acc = new_banks("h")
+        for a in range(2):
+            for g in range(PASSES):
                 for t in range(PACK):
-                    product_pass(g_acc[a][t], pairs, g, t, halves[a])
+                    product_pass(h_acc[a][t], w2_pairs[g], g, t, a)
 
-        feat_b = []
-        for t in range(PACK):
-            piece = keep.tile([P, HALF], F32, name=f"feat_b{t}", tag=f"w1_{t // 2}_{t % 2}", align_bytes=64)
-            nc.sync.dma_start(piece[:], feat_rows[:, t, halves[1]])
-            feat_b.append(piece[:])
+        out_rows = out_0.rearrange("(p t) s -> p t s", t=PACK)
+        ys = []
+        for a in range(2):
+            ys.append(new_tile([P, PACK, HALF], F32, f"y{a}"))
+            for t in range(PACK):
+                u = new_tile([P, HALF], F32, f"u{a}{t}")
+                nc.vector.tensor_tensor(u[:], h_acc[a][t][:], scaled[a][t], ADD)
+                nc.scalar.activation(ys[a][:, t, :], u[:], GELU)
+                nc.sync.dma_start(out_rows[:, t, halves[a]], ys[a][:, t, :])
 
-        scaled_a = keep.tile([P, PACK, HALF], F32, name="scaled_a")
-
-        ones = keep.tile([P, 1], F32, name="ones", tag="after_gain", align_bytes=64)
-        nc.gpsimd.memset(ones[:], 1.0)
-        gain_b = [keep.tile([P, HALF], F32, name=f"gain_b{t}") for t in range(PACK)]
-        for t in range(PACK):
-            nc.vector.scalar_tensor_tensor(scaled_a[:, t, :], g_acc[0][t][:], 1.0, feat_a[:, t, :], ADD, MULT)
-            nc.scalar.activation(gain_b[t][:], g_acc[1][t][:], IDENTITY, bias=ones[:])
-
-        w2_pairs = [quantise_weight(w2_raw[g], f"w2_{g}", ["after_modulate", "after_gain"]) for g in range(PASSES)]
-
-        y_planes = keep.tile([P, S], U8, name="y_planes", align_bytes=64)
+        y_plane = new_tile([P, S], U8, "y_plane")
         words_out = out_1[0].rearrange("p c r -> p (c r)").bitcast(I32)
 
-        def shift_products():
-            h_acc = [
-                [psum.tile([P, HALF], F32, name=f"h{a}{t}", tag=f"bank{a}{t}") for t in range(PACK)] for a in range(2)
-            ]
-            for g in range(PASSES):
-                for a in range(2):
-                    for t in range(PACK):
-                        product_pass(h_acc[a][t], w2_pairs[g], g, t, halves[a])
-            return h_acc
-
-        def finish(a, h_acc):
-            y = keep.tile([P, PACK, HALF], F32, name=f"y{a}")
-            for t in range(PACK):
-                u = keep.tile([P, HALF], F32, name=f"u{a}{t}")
-                nc.vector.tensor_tensor(u[:], h_acc[t][:], scaled[a][t], ADD)
-                nc.scalar.activation(y[:, t, :], u[:], GELU)
-                nc.sync.dma_start(out_rows[:, t, halves[a]], y[:, t, :])
-            return y
-
-        def hand_on(y, first, cols, vector_cols, name):
-            width = cols.stop - cols.start
-            woven = keep.tile([P, width, PACK], BF16, name=f"woven{name}", align_bytes=64)
-            src = y[:, :, cols].rearrange("p t c -> p c t")
-            split = width - vector_cols
-            if split:
-                nc.scalar.copy(woven[:, :split, :], src[:, :split, :])
-            if vector_cols:
-                nc.vector.tensor_copy(woven[:, split:, :], src[:, split:, :])
-            y_codes = keep.tile([P, width], I32, name=f"y_codes{name}", align_bytes=64)
-            out_cols = slice(first + cols.start, first + cols.stop)
+        def hand_on(start, width, scalar_cols, tag=None):
+            y = ys[start // HALF][:, :, start % HALF : start % HALF + width]
+            woven = new_tile([P, width, PACK], BF16, f"woven{start}", tag)
+            src = y.rearrange("p t (c i) -> p c t i", i=4)
+            dst = woven[:].rearrange("p (c i) t -> p c t i", i=4)
+            split = scalar_cols // 4
+            if scalar_cols > 0:
+                nc.scalar.copy(dst[:, :split], src[:, :split])
+            if scalar_cols < width:
+                nc.vector.tensor_copy(dst[:, split:], src[:, split:])
+            y_codes = new_tile([P, width], I32, f"y_codes{start}")
+            cols = slice(start, start + width)
             nc.vector.quantize_mx(
-                out=y_codes[:].bitcast(FP8X4),
-                scales=y_planes[:, out_cols],
-                in_=woven[:].rearrange("p c t -> p (c t)"),
+                out=y_codes[:].bitcast(FP8X4), scales=y_plane[:, cols], in_=woven[:].rearrange("p c t -> p (c t)")
             )
-            nc.sync.dma_start(words_out[:, out_cols], y_codes[:])
+            nc.sync.dma_start(words_out[:, cols], y_codes[:])
 
-        scaled_b0 = keep.tile([P, HALF], F32, name="scaled_b0", tag="after_modulate", align_bytes=64)
-        nc.vector.tensor_tensor(scaled_b0[:], gain_b[0][:], feat_b[0], MULT)
-        scaled_b = keep.tile([P, PACK - 1, HALF], F32, name="scaled_b", tag="after_gain", align_bytes=64)
-        for t in range(1, PACK):
-            nc.gpsimd.tensor_tensor(scaled_b[:, t - 1, :], gain_b[t][:], feat_b[t], MULT)
-        scaled = [[scaled_a[:, t, :] for t in range(PACK)], [scaled_b0[:]] + [scaled_b[:, t, :] for t in range(PACK - 1)]]
-        h_acc = shift_products()
-        y_a = finish(0, h_acc[0])
-        y_b = finish(1, h_acc[1])
-        hand_on(y_a, 0, slice(0, HALF), HALF, "a")
-        hand_on(y_b, HALF, slice(0, 256), 0, "b0")
-        hand_on(y_b, HALF, slice(256, HALF), 128, "b1")
+        hand_on(0, HALF, 0, "w2_1_dealt1")
+        hand_on(HALF, QUARTER, QUARTER)
+        hand_on(HALF + QUARTER, QUARTER, QUARTER // 2)
         for q in range(4):
             queue = nc.sync if q % 2 else nc.scalar
-            queue.dma_start(
-                out_2[0, 4 * q : 4 * q + 4, :].bitcast(I32), y_planes[32 * q : 32 * q + 4, :].bitcast(I32)
-            )
+            queue.dma_start(out_2[0, 4 * q : 4 * q + 4, :].bitcast(I32), y_plane[32 * q : 32 * q + 4, :].bitcast(I32))

@@ -21,6 +21,7 @@ P = 128
 PACK = 4
 K_PASS = P * PACK
 PASSES = K // K_PASS
+QUADRANTS = 4
 HALF = S // 2
 QUARTER = S // 4
 
@@ -33,166 +34,160 @@ def tile_picked_zfilm_gelu_po_kernel(
         sbuf = ctx.enter_context(tc.tile_pool(name="sbuf", bufs=1))
         psum = ctx.enter_context(tc.psum_pool(name="psum", bufs=1))
 
-        def new_tile(shape, dtype, name, tag=None):
-            return sbuf.tile(shape, dtype, name=name, tag=tag or name, align_bytes=64)
+        def new_tile(shape, dtype, name, reuses=None):
+            return sbuf.tile(shape, dtype, name=name, tag=reuses or name, align_bytes=64)
 
         offsets = new_tile([P, S // 16], U16, "offsets")
         nc.sync.dma_start(offsets[:], offs)
 
-        warm_in = new_tile([P, 8], F32, "warm_in")
-        warm_out = new_tile([P, 8], F32, "warm_out")
-        nc.gpsimd.memset(warm_in[:], 0.0)
-        nc.scalar.activation(warm_out[:], warm_in[:], GELU)
-
         scale_table = new_tile([P, T], U8, "scale_table")
-        nc.sync.dma_start(scale_table[0:32, :].bitcast(I32), x_scales.rearrange("g q c -> (g q) c").bitcast(I32))
+        nc.sync.dma_start(scale_table[0:32, :].bitcast(I32), x_scales.rearrange("o b c -> (o b) c").bitcast(I32))
         nc.vector.memset(scale_table[32:64, :].bitcast(I32), 0)
         nc.vector.memset(scale_table[64:P, :].bitcast(I32), 0)
         picked_rows = new_tile([P, S], U8, "picked_rows")
         nc.vector.tensor_copy(picked_rows[:], scale_table[:].indirect(offsets[:]))
-        x_planes = [new_tile([P, S], U8, f"x_plane{g}") for g in range(PASSES)]
+
+        x_planes = [new_tile([P, S], U8, f"x_plane{o}") for o in range(PASSES)]
         for plane in x_planes:
             nc.gpsimd.memset(plane[:].bitcast(I32), 0)
-        for g, queue in enumerate((nc.scalar, nc.gpsimd)):
-            for q in range(4):
-                first = 16 * g + 4 * q
+        for o, queue in enumerate((nc.scalar, nc.gpsimd)):
+            for q in range(QUADRANTS):
+                first = 16 * o + 4 * q
                 queue.dma_start(
-                    x_planes[g][32 * q : 32 * q + 4, :].bitcast(I32), picked_rows[first : first + 4, :].bitcast(I32)
+                    x_planes[o][32 * q : 32 * q + 4, :].bitcast(I32), picked_rows[first : first + 4, :].bitcast(I32)
                 )
 
-        def load_weight(w, g, name):
+        def load_weight(w, o, name):
             raw = new_tile([P, PACK, N], F32, name)
-            nc.sync.dma_start(raw[:], w[g * K_PASS : (g + 1) * K_PASS, :].rearrange("(p j) c -> p j c", j=PACK))
+            nc.sync.dma_start(raw[:], w[o * K_PASS : (o + 1) * K_PASS, :].rearrange("(p j) c -> p j c", j=PACK))
             return raw
 
-        def deal(raw, u, name):
+        def deal(raw, pair, name):
             dealt = new_tile([P, 2, P, PACK], BF16, name)
-            src = raw[:].rearrange("p j (m t) -> p m j t", t=PACK)[:, :, :, 2 * u : 2 * u + 2]
-            copy = nc.scalar.copy if u else nc.vector.tensor_copy
-            copy(dealt[:].rearrange("p t m j -> p m j t"), src)
+            src = raw[:].rearrange("p j (m t) -> p m j t", t=PACK)[:, :, :, 2 * pair : 2 * pair + 2]
+            copy = nc.scalar.copy if pair else nc.vector.tensor_copy
+            copy(dealt[:].rearrange("p s m j -> p m j s"), src)
             return dealt
 
-        def quantise(dealt, name, tag=None):
-            codes = new_tile([P, 2 * P], U32, f"{name}_codes", tag)
+        def quantise(dealt, name, reuses=None):
+            codes = new_tile([P, 2 * P], U32, f"{name}_codes", reuses)
             plane = new_tile([P, 2 * P], U8, f"{name}_plane")
             nc.vector.quantize_mx(
-                out=codes[:].bitcast(FP8X4), scales=plane[:], in_=dealt[:].rearrange("p t m j -> p (t m j)")
+                out=codes[:].bitcast(FP8X4), scales=plane[:], in_=dealt[:].rearrange("p s m j -> p (s m j)")
             )
             return codes, plane
 
         def prepare(raw, name):
-            return [quantise(deal(raw, u, f"{name}_dealt{u}"), f"{name}_{u}") for u in range(2)]
+            return [quantise(deal(raw, pair, f"{name}_dealt{pair}"), f"{name}_{pair}") for pair in range(2)]
 
         halves = [slice(0, HALF), slice(HALF, S)]
+        units = [(2 * pair + s, a) for pair in range(2) for a in range(2) for s in range(2)]
+        early, late = units[:4], units[4:]
 
-        def product_pass(acc, pairs, g, t, a):
+        def product_pass(acc, pairs, o, t, a):
             codes, plane = pairs[t // 2]
             m = slice((t % 2) * P, (t % 2 + 1) * P)
             nc.tensor.matmul_mx(
                 out=acc[:],
                 lhsT=codes[:, m].bitcast(FP8X4),
                 lhsT_scale=plane[:, m],
-                rhs=x_codes[g][:, halves[a]].bitcast(FP8X4),
-                rhs_scale=x_planes[g][:, halves[a]],
-                start=(g == 0),
-                stop=(g == PASSES - 1),
+                rhs=x_codes[o][:, halves[a]].bitcast(FP8X4),
+                rhs_scale=x_planes[o][:, halves[a]],
+                start=(o == 0),
+                stop=(o == PASSES - 1),
             )
 
         def new_banks(name):
-            return [
-                [psum.tile([P, HALF], F32, name=f"{name}{a}{t}", tag=f"bank{a}{t}") for t in range(PACK)]
-                for a in range(2)
-            ]
+            return {(t, a): psum.tile([P, HALF], F32, name=f"{name}{t}{a}", tag=f"bank{t}{a}") for t, a in units}
 
         x_codes, w1_raw = [], []
-        for g in range(PASSES):
-            table = new_tile([P, T], I32, f"word_table{g}")
-            nc.sync.dma_start(table[:], x_words[g].rearrange("p c r -> p (c r)").bitcast(I32))
-            w1_raw.append(load_weight(w1, g, f"w1_raw{g}"))
-            picked = new_tile([P, S], U32, f"x_codes{g}")
+        for o in range(PASSES):
+            table = new_tile([P, T], I32, f"word_table{o}")
+            nc.sync.dma_start(table[:], x_words[o].rearrange("p c j -> p (c j)").bitcast(I32))
+            w1_raw.append(load_weight(w1, o, f"w1_raw{o}"))
+            picked = new_tile([P, S], U32, f"x_codes{o}")
             nc.vector.tensor_copy(picked[:], table[:].bitcast(U32).indirect(offsets[:]))
             x_codes.append(picked)
 
         feat_rows = feat.rearrange("(p t) s -> p t s", t=PACK)
 
-        def load_feat(a):
-            pieces = [new_tile([P, HALF], F32, f"feat{a}{t}") for t in range(PACK)]
-            for t in range(PACK):
-                nc.sync.dma_start(pieces[t][:], feat_rows[:, t, halves[a]])
-            return pieces
+        def load_feat(t):
+            rows = new_tile([P, S], F32, f"feat{t}")
+            nc.sync.dma_start(rows[:], feat_rows[:, t, :])
+            return rows
 
         w2_raw, feats = [], []
-        for g in range(PASSES):
-            w2_raw.append(load_weight(w2, g, f"w2_raw{g}"))
-            feats.append(load_feat(g))
+        for o in range(PASSES):
+            w2_raw.append(load_weight(w2, o, f"w2_raw{o}"))
+            feats.extend(load_feat(t) for t in (2 * o, 2 * o + 1))
 
         g_acc = new_banks("g")
-        for g in range(PASSES):
-            pairs = prepare(w1_raw[g], f"w1_{g}")
-            for t in range(PACK):
-                for a in range(2):
-                    product_pass(g_acc[a][t], pairs, g, t, a)
+        for o in range(PASSES):
+            w1_pairs = prepare(w1_raw[o], f"w1_{o}")
+            for t, a in units:
+                product_pass(g_acc[t, a], w1_pairs, o, t, a)
 
         w2_pairs = [prepare(w2_raw[0], "w2_0")]
 
-        scaled_a = new_tile([P, PACK, HALF], F32, "scaled_a")
-        gains = [new_tile([P, HALF], F32, f"gain{t}") for t in range(PACK)]
-        for t in range(PACK):
-            nc.vector.scalar_tensor_tensor(scaled_a[:, t, :], g_acc[0][t][:], 1.0, feats[0][t][:], ADD, MULT)
-            nc.scalar.activation(gains[t][:], g_acc[1][t][:], IDENTITY, bias=1.0)
+        scaled, gains = {}, {}
+        for t, a in early:
+            scaled[t, a] = new_tile([P, HALF], F32, f"scaled{t}{a}")[:]
+            nc.vector.scalar_tensor_tensor(scaled[t, a], g_acc[t, a][:], 1.0, feats[t][:, halves[a]], ADD, MULT)
+        for t, a in late:
+            gains[t, a] = new_tile([P, HALF], F32, f"gain{t}{a}")
+            nc.scalar.activation(gains[t, a][:], g_acc[t, a][:], IDENTITY, bias=1.0)
 
-        dealt = [deal(w2_raw[1], u, f"w2_1_dealt{u}") for u in range(2)]
+        dealt = [deal(w2_raw[1], pair, f"w2_1_dealt{pair}") for pair in range(2)]
         first_pair = quantise(dealt[0], "w2_1_0")
-        scaled_b0 = new_tile([P, HALF], F32, "scaled_b0", "w2_1_dealt0")
-        nc.vector.tensor_tensor(scaled_b0[:], gains[0][:], feats[1][0][:], MULT)
-        w2_pairs.append([first_pair, quantise(dealt[1], "w2_1_1", "gain0")])
-        scaled_b = new_tile([P, PACK - 1, HALF], F32, "scaled_b", "w2_1_dealt1")
-        for t in range(1, PACK):
-            nc.gpsimd.tensor_tensor(scaled_b[:, t - 1, :], gains[t][:], feats[1][t][:], MULT)
-        scaled = [
-            [scaled_a[:, t, :] for t in range(PACK)],
-            [scaled_b0[:]] + [scaled_b[:, t, :] for t in range(PACK - 1)],
-        ]
+        t, a = late[0]
+        scaled[t, a] = new_tile([P, HALF], F32, f"scaled{t}{a}", reuses="w2_1_dealt0")[:]
+        nc.vector.tensor_tensor(scaled[t, a], gains[t, a][:], feats[t][:, halves[a]], MULT)
+        w2_pairs.append([first_pair, quantise(dealt[1], "w2_1_1", reuses=f"gain{t}{a}")])
+        scaled_rest = new_tile([P, len(late) - 1, HALF], F32, "scaled_rest", reuses="w2_1_dealt1")
+        for i, (t, a) in enumerate(late[1:]):
+            scaled[t, a] = scaled_rest[:, i, :]
+            nc.gpsimd.tensor_tensor(scaled[t, a], gains[t, a][:], feats[t][:, halves[a]], MULT)
 
         h_acc = new_banks("h")
-        for a in range(2):
-            for g in range(PASSES):
-                for t in range(PACK):
-                    product_pass(h_acc[a][t], w2_pairs[g], g, t, a)
+        for group in (early, late):
+            for o in range(PASSES):
+                for t, a in group:
+                    product_pass(h_acc[t, a], w2_pairs[o], o, t, a)
 
         out_rows = out_0.rearrange("(p t) s -> p t s", t=PACK)
-        ys = []
-        for a in range(2):
-            ys.append(new_tile([P, PACK, HALF], F32, f"y{a}"))
-            for t in range(PACK):
-                u = new_tile([P, HALF], F32, f"u{a}{t}")
-                nc.vector.tensor_tensor(u[:], h_acc[a][t][:], scaled[a][t], ADD)
-                nc.scalar.activation(ys[a][:, t, :], u[:], GELU)
-                nc.sync.dma_start(out_rows[:, t, halves[a]], ys[a][:, t, :])
+        ys = [new_tile([P, PACK, HALF], F32, f"y{a}") for a in range(2)]
+        for t, a in units:
+            summed = new_tile([P, HALF], F32, f"summed{t}{a}")
+            nc.vector.tensor_tensor(summed[:], h_acc[t, a][:], scaled[t, a], ADD)
+            nc.scalar.activation(ys[a][:, t, :], summed[:], GELU)
+            nc.sync.dma_start(out_rows[:, t, halves[a]], ys[a][:, t, :])
 
-        y_plane = new_tile([P, S], U8, "y_plane")
-        words_out = out_1[0].rearrange("p c r -> p (c r)").bitcast(I32)
-
-        def hand_on(start, width, scalar_cols, tag=None):
-            y = ys[start // HALF][:, :, start % HALF : start % HALF + width]
-            woven = new_tile([P, width, PACK], BF16, f"woven{start}", tag)
+        def weave(first, width, scalar_width, reuses=None):
+            y = ys[first // HALF][:, :, first % HALF : first % HALF + width]
+            woven = new_tile([P, width, PACK], BF16, f"woven{first}", reuses)
             src = y.rearrange("p t (c i) -> p c t i", i=4)
             dst = woven[:].rearrange("p (c i) t -> p c t i", i=4)
-            split = scalar_cols // 4
-            if scalar_cols > 0:
+            split = scalar_width // 4
+            if scalar_width > 0:
                 nc.scalar.copy(dst[:, :split], src[:, :split])
-            if scalar_cols < width:
+            if scalar_width < width:
                 nc.vector.tensor_copy(dst[:, split:], src[:, split:])
-            y_codes = new_tile([P, width], I32, f"y_codes{start}")
-            cols = slice(start, start + width)
+            return first, width, woven
+
+        y_plane = new_tile([P, S], U8, "y_plane")
+        words_out = out_1[0].rearrange("p c t -> p (c t)").bitcast(I32)
+        for first, width, woven in [
+            weave(0, HALF, 0, reuses="w2_1_dealt1"),
+            weave(HALF, QUARTER, QUARTER),
+            weave(HALF + QUARTER, QUARTER, QUARTER // 2),
+        ]:
+            y_codes = new_tile([P, width], I32, f"y_codes{first}")
+            cols = slice(first, first + width)
             nc.vector.quantize_mx(
                 out=y_codes[:].bitcast(FP8X4), scales=y_plane[:, cols], in_=woven[:].rearrange("p c t -> p (c t)")
             )
             nc.sync.dma_start(words_out[:, cols], y_codes[:])
 
-        hand_on(0, HALF, 0, "w2_1_dealt1")
-        hand_on(HALF, QUARTER, QUARTER)
-        hand_on(HALF + QUARTER, QUARTER, QUARTER // 2)
-        for q in range(4):
+        for q in range(QUADRANTS):
             queue = nc.sync if q % 2 else nc.scalar
             queue.dma_start(out_2[0, 4 * q : 4 * q + 4, :].bitcast(I32), y_plane[32 * q : 32 * q + 4, :].bitcast(I32))

from contextlib import ExitStack

import concourse.mybir as mybir

K, T, S, N = 1024, 4096, 1024, 512
FLOPS = 2 * 2 * K * N * S

F32 = mybir.dt.float32
BF16 = mybir.dt.bfloat16
I32 = mybir.dt.int32
U32 = mybir.dt.uint32
U16 = mybir.dt.uint16
U8 = mybir.dt.uint8
FP8X4 = mybir.dt.float8_e4m3fn_x4
ADD = mybir.AluOpType.add
MULT = mybir.AluOpType.mult
IDENTITY = mybir.ActivationFunctionType.Identity
GELU = mybir.ActivationFunctionType.Gelu_apprx_tanh

P = 128
PACK = 4
K_PASS = P * PACK
PASSES = K // K_PASS
QUADRANTS = 4
HALF = S // 2
QUARTER = S // 4


def tile_picked_zfilm_gelu_po_kernel(
    tc, x_words, x_scales, w1, w2, feat, offs, out_0, out_1, out_2
):
    nc = tc.nc
    with ExitStack() as ctx:
        sbuf = ctx.enter_context(tc.tile_pool(name="sbuf", bufs=1))
        psum = ctx.enter_context(tc.psum_pool(name="psum", bufs=1))

        def new_tile(shape, dtype, name, reuses=None):
            return sbuf.tile(shape, dtype, name=name, tag=reuses or name, align_bytes=64)

        offsets = new_tile([P, S // 16], U16, "offsets")
        nc.sync.dma_start(offsets[:], offs)

        scale_table = new_tile([P, T], U8, "scale_table")
        nc.sync.dma_start(scale_table[0:32, :].bitcast(I32), x_scales.rearrange("o b c -> (o b) c").bitcast(I32))
        nc.vector.memset(scale_table[32:64, :].bitcast(I32), 0)
        nc.vector.memset(scale_table[64:P, :].bitcast(I32), 0)
        picked_rows = new_tile([P, S], U8, "picked_rows")
        nc.vector.tensor_copy(picked_rows[:], scale_table[:].indirect(offsets[:]))

        x_planes = [new_tile([P, S], U8, f"x_plane{o}") for o in range(PASSES)]
        for plane in x_planes:
            nc.gpsimd.memset(plane[:].bitcast(I32), 0)
        for o, queue in enumerate((nc.scalar, nc.gpsimd)):
            for q in range(QUADRANTS):
                first = 16 * o + 4 * q
                queue.dma_start(
                    x_planes[o][32 * q : 32 * q + 4, :].bitcast(I32), picked_rows[first : first + 4, :].bitcast(I32)
                )

        def load_weight(w, o, name):
            raw = new_tile([P, PACK, N], F32, name)
            nc.sync.dma_start(raw[:], w[o * K_PASS : (o + 1) * K_PASS, :].rearrange("(p j) c -> p j c", j=PACK))
            return raw

        def deal(raw, pair, name):
            dealt = new_tile([P, 2, P, PACK], BF16, name)
            src = raw[:].rearrange("p j (m t) -> p m j t", t=PACK)[:, :, :, 2 * pair : 2 * pair + 2]
            copy = nc.scalar.copy if pair else nc.vector.tensor_copy
            copy(dealt[:].rearrange("p s m j -> p m j s"), src)
            return dealt

        def quantise(dealt, name, reuses=None):
            codes = new_tile([P, 2 * P], U32, f"{name}_codes", reuses)
            plane = new_tile([P, 2 * P], U8, f"{name}_plane")
            nc.vector.quantize_mx(
                out=codes[:].bitcast(FP8X4), scales=plane[:], in_=dealt[:].rearrange("p s m j -> p (s m j)")
            )
            return codes, plane

        def prepare(raw, name):
            return [quantise(deal(raw, pair, f"{name}_dealt{pair}"), f"{name}_{pair}") for pair in range(2)]

        halves = [slice(0, HALF), slice(HALF, S)]
        units = [(2 * pair + s, a) for pair in range(2) for a in range(2) for s in range(2)]
        early, late = units[:4], units[4:]

        def product_pass(acc, pairs, o, t, a):
            codes, plane = pairs[t // 2]
            m = slice((t % 2) * P, (t % 2 + 1) * P)
            nc.tensor.matmul_mx(
                out=acc[:],
                lhsT=codes[:, m].bitcast(FP8X4),
                lhsT_scale=plane[:, m],
                rhs=x_codes[o][:, halves[a]].bitcast(FP8X4),
                rhs_scale=x_planes[o][:, halves[a]],
                start=(o == 0),
                stop=(o == PASSES - 1),
            )

        def new_banks(name):
            return {(t, a): psum.tile([P, HALF], F32, name=f"{name}{t}{a}", tag=f"bank{t}{a}") for t, a in units}

        x_codes, w1_raw = [], []
        for o in range(PASSES):
            table = new_tile([P, T], I32, f"word_table{o}")
            nc.sync.dma_start(table[:], x_words[o].rearrange("p c j -> p (c j)").bitcast(I32))
            w1_raw.append(load_weight(w1, o, f"w1_raw{o}"))
            picked = new_tile([P, S], U32, f"x_codes{o}")
            nc.vector.tensor_copy(picked[:], table[:].bitcast(U32).indirect(offsets[:]))
            x_codes.append(picked)

        feat_rows = feat.rearrange("(p t) s -> p t s", t=PACK)

        def load_feat(t):
            rows = new_tile([P, S], F32, f"feat{t}")
            nc.sync.dma_start(rows[:], feat_rows[:, t, :])
            return rows

        w2_raw, feats = [], []
        for o in range(PASSES):
            w2_raw.append(load_weight(w2, o, f"w2_raw{o}"))
            feats.extend(load_feat(t) for t in (2 * o, 2 * o + 1))

        g_acc = new_banks("g")
        for o in range(PASSES):
            w1_pairs = prepare(w1_raw[o], f"w1_{o}")
            for t, a in units:
                product_pass(g_acc[t, a], w1_pairs, o, t, a)

        w2_pairs = [prepare(w2_raw[0], "w2_0")]

        scaled, gains = {}, {}
        for t, a in early:
            scaled[t, a] = new_tile([P, HALF], F32, f"scaled{t}{a}")[:]
            nc.vector.scalar_tensor_tensor(scaled[t, a], g_acc[t, a][:], 1.0, feats[t][:, halves[a]], ADD, MULT)
        for t, a in late:
            gains[t, a] = new_tile([P, HALF], F32, f"gain{t}{a}")
            nc.scalar.activation(gains[t, a][:], g_acc[t, a][:], IDENTITY, bias=1.0)

        dealt = [deal(w2_raw[1], pair, f"w2_1_dealt{pair}") for pair in range(2)]
        first_pair = quantise(dealt[0], "w2_1_0")
        t, a = late[0]
        scaled[t, a] = new_tile([P, HALF], F32, f"scaled{t}{a}", reuses="w2_1_dealt0")[:]
        nc.vector.tensor_tensor(scaled[t, a], gains[t, a][:], feats[t][:, halves[a]], MULT)
        w2_pairs.append([first_pair, quantise(dealt[1], "w2_1_1", reuses=f"gain{t}{a}")])
        scaled_rest = new_tile([P, len(late) - 1, HALF], F32, "scaled_rest", reuses="w2_1_dealt1")
        for i, (t, a) in enumerate(late[1:]):
            scaled[t, a] = scaled_rest[:, i, :]
            nc.gpsimd.tensor_tensor(scaled[t, a], gains[t, a][:], feats[t][:, halves[a]], MULT)

        h_acc = new_banks("h")
        for group in (early, late):
            for o in range(PASSES):
                for t, a in group:
                    product_pass(h_acc[t, a], w2_pairs[o], o, t, a)

        out_rows = out_0.rearrange("(p t) s -> p t s", t=PACK)
        ys = [new_tile([P, PACK, HALF], F32, f"y{a}") for a in range(2)]
        for t, a in units:
            summed = new_tile([P, HALF], F32, f"summed{t}{a}")
            nc.vector.tensor_tensor(summed[:], h_acc[t, a][:], scaled[t, a], ADD)
            nc.scalar.activation(ys[a][:, t, :], summed[:], GELU)
            nc.sync.dma_start(out_rows[:, t, halves[a]], ys[a][:, t, :])

        def weave(first, width, scalar_width, reuses=None):
            y = ys[first // HALF][:, :, first % HALF : first % HALF + width]
            woven = new_tile([P, width, PACK], BF16, f"woven{first}", reuses)
            src = y.rearrange("p t (c i) -> p c t i", i=4)
            dst = woven[:].rearrange("p (c i) t -> p c t i", i=4)
            split = scalar_width // 4
            if scalar_width > 0:
                nc.scalar.copy(dst[:, :split], src[:, :split])
            if scalar_width < width:
                nc.vector.tensor_copy(dst[:, split:], src[:, split:])
            return first, width, woven

        y_plane = new_tile([P, S], U8, "y_plane")
        words_out = out_1[0].rearrange("p c t -> p (c t)").bitcast(I32)
        for first, width, woven in [
            weave(0, HALF, 0, reuses="w2_1_dealt1"),
            weave(HALF, QUARTER, QUARTER),
            weave(HALF + QUARTER, QUARTER, QUARTER // 2),
        ]:
            y_codes = new_tile([P, width], I32, f"y_codes{first}")
            cols = slice(first, first + width)
            nc.vector.quantize_mx(
                out=y_codes[:].bitcast(FP8X4), scales=y_plane[:, cols], in_=woven[:].rearrange("p c t -> p (c t)")
            )
            nc.sync.dma_start(words_out[:, cols], y_codes[:])

        for q in range(QUADRANTS):
            queue = nc.sync if q % 2 else nc.scalar
            queue.dma_start(out_2[0, 4 * q : 4 * q + 4, :].bitcast(I32), y_plane[32 * q : 32 * q + 4, :].bitcast(I32))
